import numpy as np
import ml_dtypes


def mxq(x, axis, fmt="e4m3"):
    dtype, down = {"e4m3": (ml_dtypes.float8_e4m3fn, 7), "e5m2": (ml_dtypes.float8_e5m2, 14)}[fmt]
    v = np.moveaxis(np.asarray(x, np.float32).astype(ml_dtypes.bfloat16).astype(np.float64), axis, -1)
    blocks = v.reshape(v.shape[:-1] + (-1, 32))
    amax = np.abs(blocks).max(-1, keepdims=True)
    byte = np.maximum(np.where(amax > 0, np.frexp(amax)[1] - 1 + 127, 0) - down, 1)
    scale = np.exp2(byte - 127.0)
    codes = (blocks / scale).astype(np.float32).astype(dtype).astype(np.float64)
    return np.moveaxis((codes * scale).reshape(v.shape), -1, axis)


WIDE = False


def mx_kscale(k):
    if not WIDE:
        return np.ones(k)
    levels = np.array([10, -10, 5, -5, 0])
    if k % 512:
        return np.exp2(np.random.permutation(np.resize(levels, k // 32))).repeat(32)
    a = np.empty((k // 512, 16))
    for p in range(k // 512):
        a[p, :8] = np.random.permutation(np.resize(levels, 8))
        for g in range(8):
            far = levels[np.abs(levels - a[p, g]) >= 10]
            a[p, g + 8] = far[np.random.randint(len(far))]
    return np.exp2(a.ravel()).repeat(32)


def f64(x):
    return np.asarray(x).astype(np.float64)


def striped(idx):
    return np.tile(idx.reshape(-1, 16).T, (8, 1)).astype(np.uint16)


def unstriped(offs):
    return offs[:16].T.reshape(-1).astype(np.int64)


E2M1 = np.array([0.0, 0.5, 1.0, 1.5, 2.0, 3.0, 4.0, 6.0, -0.0, -0.5, -1.0, -1.5, -2.0, -3.0, -4.0, -6.0])


def pack_weight(w, fmt):
    k, n = w.shape
    w = f64(np.asarray(w, np.float32).astype(ml_dtypes.bfloat16)).reshape(k // 32, 32, n)
    amax = np.abs(w).max(1)
    if fmt == "e4m3":
        byte = np.frexp(amax)[1] - 1 + 127 - 7
    else:
        mant, ex = np.frexp(amax / 6.0)
        byte = np.where(mant > 0.5, ex, ex - 1) + 127
    byte = np.clip(np.where(amax > 0, byte, 1), 1, 254)
    scaled = (w * np.exp2(127.0 - byte)[:, None, :]).reshape(k, n).astype(np.float32)
    by_word = np.ascontiguousarray(scaled.reshape(k // 512, 128, 4, n).transpose(0, 1, 3, 2))
    if fmt == "e4m3":
        words = by_word.astype(ml_dtypes.float8_e4m3fn).view(np.uint8)
    else:
        c = by_word.astype(ml_dtypes.float4_e2m1fn).view(np.uint8) & 0xF
        words = (c[..., 0::2] | (c[..., 1::2] << 4)).reshape(k // 512, 128, 2 * n)
    return np.ascontiguousarray(words), np.ascontiguousarray(byte.astype(np.uint8).reshape(k // 512, 16, n))


def unpack_weight(words, scales, fmt):
    g, _, n = scales.shape
    words = np.ascontiguousarray(words).reshape(g, 128, n, -1)
    if fmt == "e4m3":
        vals = words.view(ml_dtypes.float8_e4m3fn).astype(np.float64)
    else:
        nib = np.empty((g, 128, n, 4), np.uint8)
        nib[..., 0::2] = words & 0xF
        nib[..., 1::2] = words >> 4
        vals = E2M1[nib]
    vals = vals * np.repeat(np.exp2(scales.astype(np.float64) - 127.0), 8, axis=1)[..., None]
    return vals.transpose(0, 1, 3, 2).reshape(g * 512, n)


def gelu(v):
    return 0.5 * v * (1.0 + np.tanh(np.sqrt(2.0 / np.pi) * (v + 0.044715 * v**3)))


def bf(x):
    return np.asarray(x, np.float32).astype(ml_dtypes.bfloat16)


def planes(Y):
    n, m = Y.shape
    b = f64(bf(Y)).reshape(n // 32, 32, m)
    amax = np.abs(b).max(1)
    byte = np.clip(np.where(amax > 0, np.frexp(amax)[1] - 1 + 127 - 7, 1), 1, 254)
    codes = (b * np.exp2(127.0 - byte)[:, None, :]).reshape(n, m).astype(np.float32).astype(ml_dtypes.float8_e4m3fn).view(np.uint8)
    words = codes.reshape(n // 512, 128, 4, m).transpose(0, 1, 3, 2)
    return np.ascontiguousarray(words), np.ascontiguousarray(byte.astype(np.uint8).reshape(n // 512, 16, m))


K, K2, H, N, T, T3, S = 512, 1024, 1024, 512, 2048, 4096, 1024

def setup_inputs():
    n = np.random.standard_normal
    s, s2, u = mx_kscale(K)[:, None], mx_kscale(K2)[:, None], mx_kscale(H)[:, None]
    tab_words, tab_scales = pack_weight(n((K, T)) * s, "e4m3")
    tab2_words, tab2_scales = pack_weight(n((K2, T)) * s2, "e4m3")
    tab3_words, tab3_scales = pack_weight(n((K, T3)) * s, "e2m1")
    w1_words, w1_scales = pack_weight(n((K, H)) / np.sqrt(K) / s, "e2m1")
    w3_words, w3_scales = pack_weight(n((K, H)) / np.sqrt(K) / s * u.T, "e4m3")
    return {
        "tab_words": tab_words, "tab_scales": tab_scales,
        "tab2_words": tab2_words, "tab2_scales": tab2_scales,
        "tab3_words": tab3_words, "tab3_scales": tab3_scales,
        "offs": striped(np.random.permutation(T)[:S]),
        "offs2": striped(np.random.permutation(T)[:S]),
        "offs3": striped(np.random.permutation(T3)[:S]),
        "w1_words": w1_words, "w1_scales": w1_scales,
        "w2": (n((K2, H)) / np.sqrt(K2) / s2).astype(np.float32),
        "w3_words": w3_words, "w3_scales": w3_scales,
        "meas": (n((H, S)) * u).astype(np.float32),
        "w4": (0.5 * n((H, N)) / np.sqrt(H) / u).astype(np.float32),
        "step": np.exp(0.8 * n(N)).astype(np.float32),
    }

def reference(tab_words, tab_scales, tab2_words, tab2_scales, tab3_words, tab3_scales, offs, offs2, offs3,
              w1_words, w1_scales, w2, w3_words, w3_scales, meas, w4, step):
    v = unpack_weight(tab_words, tab_scales, "e4m3")[:, unstriped(offs)]
    v2 = unpack_weight(tab2_words, tab2_scales, "e4m3")[:, unstriped(offs2)]
    v3 = unpack_weight(tab3_words, tab3_scales, "e2m1")[:, unstriped(offs3)]
    seed = unpack_weight(w1_words, w1_scales, "e2m1").T @ v
    soil = mxq(f64(w2), 0, "e4m3").T @ v2
    rain = unpack_weight(w3_words, w3_scales, "e4m3").T @ v3
    resid = seed * soil * rain - f64(meas)
    z = resid * seed
    y = f64(step)[:, None] * (mxq(f64(w4), 0, "e4m3").T @ mxq(z, 0, "e4m3"))
    words, scales = planes(y)
    return y, words, scales

@@ -1,0 +1,286 @@
+from contextlib import ExitStack
+
+import concourse.mybir as mybir
+
+K, K2, H, N, T, T3, S = 512, 1024, 1024, 512, 2048, 4096, 1024
+FLOPS = 2 * S * (K * H + K2 * H + K * H + H * N)
+
+F32 = mybir.dt.float32
+BF16 = mybir.dt.bfloat16
+I32 = mybir.dt.int32
+U32 = mybir.dt.uint32
+U16 = mybir.dt.uint16
+U8 = mybir.dt.uint8
+FP8X4 = mybir.dt.float8_e4m3fn_x4
+FP4X4 = mybir.dt.float4_e2m1fn_x4
+MULT = mybir.AluOpType.mult
+SUB = mybir.AluOpType.subtract
+SQUARE = mybir.ActivationFunctionType.Square
+COPY = mybir.ActivationFunctionType.Copy
+
+P = 128
+PACK = 4
+KP = P * PACK
+HALF = 512
+STEP = 128
+LAG = 1
+Y_CHUNKS = (256, 256, 256, 128, 128)
+
+
+def tile_list_rice_factor_refit_kernel(
+    tc, tab_words, tab_scales, tab2_words, tab2_scales, tab3_words, tab3_scales, offs, offs2, offs3,
+    w1_words, w1_scales, w2, w3_words, w3_scales, meas, w4, step, out_0, out_1, out_2,
+):
+    nc = tc.nc
+    with ExitStack() as ctx:
+        keep = ctx.enter_context(tc.tile_pool(name="keep", bufs=1))
+        ring = ctx.enter_context(tc.tile_pool(name="ring", bufs=2))
+        psum = ctx.enter_context(tc.psum_pool(name="psum", bufs=1))
+
+        def held(name, width, dtype):
+            return keep.tile([P, width], dtype, name=name, align_bytes=64)
+
+        idx1 = keep.tile([P, S // 16], U16, name="idx1")
+        idx2 = keep.tile([P, S // 16], U16, name="idx2")
+        idx3 = keep.tile([P, S // 16], U16, name="idx3")
+
+        def slot(tag, name, shape, dtype):
+            return ring.tile(shape, dtype, name=name, tag=tag, bufs=1, align_bytes=64)
+
+        tab_w = slot("C", "tab_w", [P, T], I32)
+        tab2_w = [slot("EF"[a], "tab2_w", [P, T], I32) for a in range(2)]
+        tab3_w = slot("D", "tab3_w", [P, T3 // 2], I32)
+        tab_s = slot("J", "tab_s", [P, T], U8)
+        tab2_s = slot("L", "tab2_s", [P, T], U8)
+        tab3_s = slot("K", "tab3_s", [P, T3], U8)
+        w1_raw = slot("A", "w1_raw", [P, H // 2], I32)
+        w3_raw = slot("B", "w3_raw", [P, H], I32)
+        ws_raw = slot("M", "ws_raw", [P, 2 * H], U8)
+        w1_c = held("w1_c", 2 * H, U8)
+        w3_c = held("w3_c", H, I32)
+        step_t = held("step_t", PACK, F32)
+
+        for plane in (tab_s, ws_raw, tab3_s, tab2_s):
+            nc.vector.memset(plane[:].bitcast(I32), 0)
+
+        def load_scale_rows(queue, plane, rows):
+            for q in range(4):
+                queue.dma_start(out=plane[32 * q : 32 * q + 4, :].bitcast(I32), in_=rows[4 * q : 4 * q + 4, :].bitcast(I32))
+
+        def words(ap):
+            return ap.rearrange("p n t -> p (n t)").bitcast(I32)
+
+        def load_rows(src, row0, col0, tag):
+            raw = slot(tag, "rows", [P, PACK, HALF], F32)
+            nc.sync.dma_start(out=raw[:], in_=src[row0 : row0 + KP, col0 : col0 + HALF].rearrange("(p i) c -> p i c", i=PACK))
+            return raw
+
+        w2_raw, w4_raw, meas_t = {}, {}, {}
+        nc.sync.dma_start(out=w1_raw[:], in_=w1_words[0].bitcast(I32))
+        nc.sync.dma_start(out=w3_raw[:], in_=words(w3_words[0]))
+        nc.sync.dma_start(idx1[:], offs)
+        nc.sync.dma_start(out=tab_w[:], in_=words(tab_words[0]))
+        load_scale_rows(nc.sync, tab_s, tab_scales[0])
+        load_scale_rows(nc.gpsimd, ws_raw[:, 0:H], w1_scales[0])
+        load_scale_rows(nc.gpsimd, ws_raw[:, H : 2 * H], w3_scales[0])
+        nc.sync.dma_start(idx3[:], offs3)
+        nc.sync.dma_start(out=tab3_w[:], in_=tab3_words[0].bitcast(I32))
+        load_scale_rows(nc.sync, tab3_s, tab3_scales[0])
+        nc.sync.dma_start(idx2[:], offs2)
+        nc.sync.dma_start(out=tab2_w[0][:], in_=words(tab2_words[0]))
+        for q in range(4):
+            nc.sync.dma_start(out=tab2_s[32 * q : 32 * q + 8, :].bitcast(I32), in_=tab2_scales[:, 4 * q : 4 * q + 4, :].bitcast(I32))
+        nc.sync.dma_start(out=tab2_w[1][:], in_=words(tab2_words[1]))
+        nc.sync.dma_start(out=step_t[:], in_=step.rearrange("(p t) -> p t", t=PACK))
+
+        nc.vector.tensor_copy(
+            out=w1_c[:].bitcast(U16).rearrange("p (b t m) -> p b t m", b=2, t=PACK),
+            in_=w1_raw[:].bitcast(U16).rearrange("p (b m t) -> p b t m", b=2, t=PACK),
+        )
+        nc.vector.tensor_copy(
+            out=w3_c[:].rearrange("p (b t m i) -> p b m t i", b=2, t=PACK, i=4),
+            in_=w3_raw[:].rearrange("p (b m i t) -> p b m t i", b=2, t=PACK, i=4),
+        )
+
+        v_w = [held("v_w%d" % h, HALF, U32) for h in range(2)]
+        v2_w = [[held("v2_w%d_%d" % (h, a), HALF, U32) for a in range(2)] for h in range(2)]
+        v3_w = [held("v3_w%d" % h, HALF, U16) for h in range(2)]
+
+        def gather(dst, window, idx, h):
+            cols = HALF // 16
+            nc.vector.tensor_copy(dst, window.indirect(idx[:, h * cols : (h + 1) * cols]))
+
+        w2_s = [[held("w2_s%d_%d" % (b, a), HALF, U8) for a in range(2)] for b in range(2)]
+        w4_c = [held("w4_c%d" % b, N, U32) for b in range(2)]
+        w4_s = [held("w4_s%d" % b, N, U8) for b in range(2)]
+
+        def round_weight(raw, tag):
+            grouped = slot(tag, "w_bf", [P, PACK * HALF], BF16)
+            for m in (slice(0, P // 2), slice(P // 2, P)):
+                nc.scalar.copy(
+                    out=grouped[:].rearrange("p (t m i) -> p m t i", t=PACK, i=PACK)[:, m],
+                    in_=raw[:].rearrange("p i (m t) -> p m t i", t=PACK)[:, m],
+                )
+            return grouped
+
+        def quantise(codes, scales, grouped):
+            nc.vector.quantize_mx(out=codes.bitcast(FP8X4), scales=scales, in_=grouped)
+
+        w2_raw[0, 0] = load_rows(w2, 0, 0, "A")
+        w2_raw[0, 1] = load_rows(w2, KP, 0, "B")
+        for h in range(2):
+            gather(v_w[h][:], tab_w[:].bitcast(U32), idx1, h)
+        meas_t[0, 0] = load_rows(meas, 0, 0, "C")
+        for h in range(2):
+            gather(v3_w[h][:], tab3_w[:].bitcast(U16), idx3, h)
+        meas_t[1, 0] = load_rows(meas, 0, HALF, "D")
+        for h in range(2):
+            gather(v2_w[h][0][:], tab2_w[0][:].bitcast(U32), idx2, h)
+        w2_raw[1, 0] = load_rows(w2, 0, HALF, "E")
+        for h in range(2):
+            gather(v2_w[h][1][:], tab2_w[1][:].bitcast(U32), idx2, h)
+        picked_s = slot("F", "picked_s", [P, 3 * S], U8)
+        v_s, v3_s, v2_s = [[picked_s[:, n * S + h * HALF : n * S + (h + 1) * HALF] for h in range(2)] for n in range(3)]
+        gather(v_s[0], tab_s[:], idx1, 0)
+        gather(v3_s[0], tab3_s[:], idx3, 0)
+        gather(v2_s[0], tab2_s[:], idx2, 0)
+        gather(v_s[1], tab_s[:], idx1, 1)
+        ws = slot("J", "ws", [P, 2 * H], U8)
+        nc.vector.tensor_copy(
+            out=ws[:].rearrange("p (b t m) -> p b t m", b=4, t=PACK),
+            in_=ws_raw[:].rearrange("p (b m t) -> p b t m", b=4, t=PACK),
+        )
+        w2_c = [[slot("M", "w2_c", [P, HALF], U32)], [held("w2_c%d" % a, HALF, U32) for a in range(2)]]
+        quantise(w2_c[0][0][:], w2_s[0][0][:], round_weight(w2_raw[0, 0], "G")[:])
+        w2_raw[1, 1] = load_rows(w2, KP, HALF, "A")
+        gather(v3_s[1], tab3_s[:], idx3, 1)
+        w2_c[0].append(slot("K", "w2_c", [P, HALF], U32))
+        quantise(w2_c[0][1][:], w2_s[0][1][:], round_weight(w2_raw[0, 1], "H")[:])
+        meas_t[0, 1] = load_rows(meas, KP, 0, "B")
+        gather(v2_s[1], tab2_s[:], idx2, 1)
+        w4_raw[0] = load_rows(w4, 0, 0, "L")
+
+        z_c = [[held("z_c%d_%d" % (h, b), HALF, U32) for b in range(2)] for h in range(2)]
+        z_s = [[held("z_s%d_%d" % (h, b), HALF, U8) for b in range(2)] for h in range(2)]
+        y_c = held("y_c", S, U32)
+        y_s = held("y_s", S, U8)
+        z_bf = {}
+
+        def woven(bank):
+            return bank[:].rearrange("p t j -> p j t")
+
+        def as_woven(flat):
+            return flat.rearrange("p (j t) -> p j t", t=PACK)
+
+        def first_products(i, h, b, c):
+            cols = slice(c * STEP, (c + 1) * STEP)
+            soil = psum.tile([P, PACK, STEP], F32, name="soil", tag="soil", bufs=2)
+            rain = psum.tile([P, PACK, STEP], F32, name="rain", tag="rain", bufs=2)
+            seed = psum.tile([P, PACK, STEP], F32, name="seed", tag="seed", bufs=2)
+            for t in range(PACK):
+                r0 = b * KP + t * P
+                nc.tensor.matmul_mx(
+                    out=seed[:, t, :], lhsT=w1_c[:, 2 * r0 : 2 * (r0 + P)].bitcast(FP4X4), lhsT_scale=ws[:, r0 : r0 + P],
+                    rhs=v_w[h][:, cols].bitcast(FP8X4), rhs_scale=v_s[h][:, cols], start=True, stop=True,
+                )
+            for t in range(PACK):
+                wc = slice(t * P, (t + 1) * P)
+                for a in range(2):
+                    nc.tensor.matmul_mx(
+                        out=soil[:, t, :], lhsT=w2_c[b][a][:, wc].bitcast(FP8X4), lhsT_scale=w2_s[b][a][:, wc],
+                        rhs=v2_w[h][a][:, cols].bitcast(FP8X4), rhs_scale=v2_s[h][4 * a : P, cols],
+                        start=(a == 0), stop=(a == 1),
+                    )
+            for t in range(PACK):
+                r0 = b * KP + t * P
+                nc.tensor.matmul_mx(
+                    out=rain[:, t, :], lhsT=w3_c[:, r0 : r0 + P].bitcast(FP8X4), lhsT_scale=ws[:, H + r0 : H + r0 + P],
+                    rhs=v3_w[h][:, cols].bitcast(FP4X4), rhs_scale=v3_s[h][:, cols], start=True, stop=True,
+                )
+            square = ring.tile([P, PACK * STEP], F32, name="square", tag="square", bufs=3)
+            nc.scalar.activation(out=as_woven(square[:]), in_=woven(seed), func=SQUARE)
+            both = slot("GH"[i // 2 % 2] if i % 2 == 0 else "I", "both", [P, PACK * STEP], F32)
+            nc.vector.tensor_tensor(out=as_woven(both[:]), in0=woven(soil), in1=as_woven(square[:]), op=MULT)
+            minus = ring.tile([P, PACK, STEP], F32, name="minus", tag="minus", bufs=3)
+            nc.vector.tensor_tensor(out=minus[:], in0=seed[:], in1=meas_t[h, b][:, :, cols], op=MULT)
+            plus = ring.tile([P, PACK * STEP], F32, name="plus", tag="plus", bufs=3)
+            nc.vector.tensor_tensor(out=as_woven(plus[:]), in0=woven(rain), in1=as_woven(both[:]), op=MULT)
+            if c == 0:
+                z_bf[h, b] = ring.tile([P, PACK * HALF], BF16, name="z_bf", tag="z_bf", bufs=2, align_bytes=64)
+            engine = nc.vector if i == len(steps) - 1 else nc.gpsimd
+            engine.tensor_tensor(
+                out=as_woven(z_bf[h, b][:, c * KP : (c + 1) * KP]), in0=as_woven(plus[:]), in1=woven(minus), op=SUB,
+            )
+
+        def quantise_z(h, b, c0, width):
+            cols = slice(c0, c0 + width)
+            quantise(z_c[h][b][:, cols], z_s[h][b][:, cols], z_bf[h, b][:, PACK * c0 : PACK * (c0 + width)])
+
+        y_tiles = {}
+        store_of = {}
+        j0 = 0
+        for width in Y_CHUNKS:
+            for j in range(j0, j0 + width, STEP):
+                store_of[j] = (j0, width)
+            j0 = j0 + width
+
+        def last_product(h, c):
+            cols = slice(c * STEP, (c + 1) * STEP)
+            j = h * HALF + c * STEP
+            j0, width = store_of[j]
+            if j == j0:
+                y_tiles[j0] = ring.tile([P, PACK, width], F32, name="y", tag="y", bufs=2)
+            y = y_tiles[j0][:, :, j - j0 : j - j0 + STEP]
+            bank = psum.tile([P, PACK, STEP], F32, name="y_bank", tag="y_bank", bufs=2)
+            for t in range(PACK):
+                wc = slice(t * P, (t + 1) * P)
+                for b in range(2):
+                    nc.tensor.matmul_mx(
+                        out=bank[:, t, :], lhsT=w4_c[b][:, wc].bitcast(FP8X4), lhsT_scale=w4_s[b][:, wc],
+                        rhs=z_c[h][b][:, cols].bitcast(FP8X4), rhs_scale=z_s[h][b][:, cols],
+                        start=(b == 0), stop=(b == 1),
+                    )
+            for t in range(PACK):
+                nc.scalar.activation(out=y[:, t, :], in_=bank[:, t, :], func=COPY, scale=step_t[:, t : t + 1])
+            if j + STEP == j0 + width:
+                nc.sync.dma_start(out=out_0[:, j0 : j0 + width].rearrange("(p t) j -> p t j", t=PACK), in_=y_tiles[j0][:])
+            y_bf = ring.tile([P, PACK * STEP], BF16, name="y_bf", tag="y_bf", bufs=2, align_bytes=64)
+            if j + 2 * STEP >= S:
+                nc.vector.tensor_copy(out=as_woven(y_bf[:]), in_=y.rearrange("p t j -> p j t"))
+            else:
+                nc.scalar.copy(out=as_woven(y_bf[:]), in_=y.rearrange("p t j -> p j t"))
+            return j, y_bf
+
+        def planes(j, y_bf):
+            quantise(y_c[:, j : j + STEP], y_s[:, j : j + STEP], y_bf[:])
+            j0, width = store_of[j]
+            if j + STEP == j0 + width:
+                nc.sync.dma_start(out=words(out_1[0])[:, j0 : j0 + width], in_=y_c[:, j0 : j0 + width].bitcast(I32))
+
+        steps = [(h, b, c) for b in range(2) for h in range(2) for c in range(HALF // STEP)]
+        rounded = {}
+        for i in range(len(steps) + LAG + 2):
+            if i < len(steps):
+                first_products(i, *steps[i])
+            if i in (0, 2):
+                a = i // 2
+                quantise(w2_c[1][a][:], w2_s[1][a][:], round_weight(w2_raw[1, a], "GH"[a])[:])
+            if i == 0:
+                w4_raw[1] = load_rows(w4, KP, 0, "E")
+            if i == 2:
+                meas_t[1, 1] = load_rows(meas, KP, HALF, "A")
+            if i in (4, 6):
+                a = i // 2 - 2
+                quantise(w4_c[a][:], w4_s[a][:], round_weight(w4_raw[a], "GH"[a])[:])
+            n = i - LAG
+            if n - 2 in rounded:
+                planes(*rounded[n - 2])
+            if 1 <= n <= len(steps):
+                h, b, c = steps[n - 1]
+                if b == 0 and c == HALF // STEP - 1:
+                    quantise_z(h, 0, 0, HALF)
+                if b == 1:
+                    quantise_z(h, 1, c * STEP, STEP)
+                    rounded[n - 1] = last_product(h, c)
+        for q in range(4):
+            nc.sync.dma_start(out=out_2[0, 4 * q : 4 * q + 4, :].bitcast(I32), in_=y_s[32 * q : 32 * q + 4, :].bitcast(I32))

@@ -23,8 +23,9 @@ PACK = 4
 KP = P * PACK
 HALF = 512
 STEP = 128
-LAG = 1
-Y_CHUNKS = (256, 256, 256, 128, 128)
+QUARTER = 256
+CHUNKS = S // STEP
+Y_STORES = (256, 256, 256, 128, 128)
 
 
 def tile_list_rice_factor_refit_kernel(
@@ -47,186 +48,192 @@ def tile_list_rice_factor_refit_kernel(
         def slot(tag, name, shape, dtype):
             return ring.tile(shape, dtype, name=name, tag=tag, bufs=1, align_bytes=64)
 
-        tab_w = slot("C", "tab_w", [P, T], I32)
-        tab2_w = [slot("EF"[a], "tab2_w", [P, T], I32) for a in range(2)]
-        tab3_w = slot("D", "tab3_w", [P, T3 // 2], I32)
-        tab_s = slot("J", "tab_s", [P, T], U8)
-        tab2_s = slot("L", "tab2_s", [P, T], U8)
-        tab3_s = slot("K", "tab3_s", [P, T3], U8)
-        w1_raw = slot("A", "w1_raw", [P, H // 2], I32)
-        w3_raw = slot("B", "w3_raw", [P, H], I32)
-        ws_raw = slot("M", "ws_raw", [P, 2 * H], U8)
-        w1_c = held("w1_c", 2 * H, U8)
-        w3_c = held("w3_c", H, I32)
-        step_t = held("step_t", PACK, F32)
+        def words(ap):
+            return ap.rearrange("p n t -> p (n t)").bitcast(I32)
 
-        for plane in (tab_s, ws_raw, tab3_s, tab2_s):
-            nc.vector.memset(plane[:].bitcast(I32), 0)
+        def load_words(tag, src):
+            raw = slot(tag, "packed", [P, src.shape[1]], I32)
+            nc.sync.dma_start(out=raw[:], in_=src)
+            return raw
+
+        def load_rows(tag, src, row0, col0):
+            raw = slot(tag, "rows", [P, PACK, HALF], F32)
+            nc.sync.dma_start(out=raw[:], in_=src[row0 : row0 + KP, col0 : col0 + HALF].rearrange("(p i) c -> p i c", i=PACK))
+            return raw
+
+        def load_meas(tag, col0):
+            raw = slot(tag, "meas_t", [P, 2, PACK, QUARTER], F32)
+            for b in range(2):
+                rows = meas[b * KP : (b + 1) * KP, col0 : col0 + QUARTER]
+                nc.sync.dma_start(out=raw[:, b], in_=rows.rearrange("(p t) j -> p t j", t=PACK))
+            return raw
 
         def load_scale_rows(queue, plane, rows):
             for q in range(4):
                 queue.dma_start(out=plane[32 * q : 32 * q + 4, :].bitcast(I32), in_=rows[4 * q : 4 * q + 4, :].bitcast(I32))
 
-        def words(ap):
-            return ap.rearrange("p n t -> p (n t)").bitcast(I32)
+        def gather(dst, window, idx):
+            nc.vector.tensor_copy(dst, window.indirect(idx))
 
-        def load_rows(src, row0, col0, tag):
-            raw = slot(tag, "rows", [P, PACK, HALF], F32)
-            nc.sync.dma_start(out=raw[:], in_=src[row0 : row0 + KP, col0 : col0 + HALF].rearrange("(p i) c -> p i c", i=PACK))
-            return raw
-
-        w2_raw, w4_raw, meas_t = {}, {}, {}
-        nc.sync.dma_start(out=w1_raw[:], in_=w1_words[0].bitcast(I32))
-        nc.sync.dma_start(out=w3_raw[:], in_=words(w3_words[0]))
-        nc.sync.dma_start(idx1[:], offs)
-        nc.sync.dma_start(out=tab_w[:], in_=words(tab_words[0]))
-        load_scale_rows(nc.sync, tab_s, tab_scales[0])
-        load_scale_rows(nc.gpsimd, ws_raw[:, 0:H], w1_scales[0])
-        load_scale_rows(nc.gpsimd, ws_raw[:, H : 2 * H], w3_scales[0])
-        nc.sync.dma_start(idx3[:], offs3)
-        nc.sync.dma_start(out=tab3_w[:], in_=tab3_words[0].bitcast(I32))
-        load_scale_rows(nc.sync, tab3_s, tab3_scales[0])
-        nc.sync.dma_start(idx2[:], offs2)
-        nc.sync.dma_start(out=tab2_w[0][:], in_=words(tab2_words[0]))
-        for q in range(4):
-            nc.sync.dma_start(out=tab2_s[32 * q : 32 * q + 8, :].bitcast(I32), in_=tab2_scales[:, 4 * q : 4 * q + 4, :].bitcast(I32))
-        nc.sync.dma_start(out=tab2_w[1][:], in_=words(tab2_words[1]))
-        nc.sync.dma_start(out=step_t[:], in_=step.rearrange("(p t) -> p t", t=PACK))
-
-        nc.vector.tensor_copy(
-            out=w1_c[:].bitcast(U16).rearrange("p (b t m) -> p b t m", b=2, t=PACK),
-            in_=w1_raw[:].bitcast(U16).rearrange("p (b m t) -> p b t m", b=2, t=PACK),
-        )
-        nc.vector.tensor_copy(
-            out=w3_c[:].rearrange("p (b t m i) -> p b m t i", b=2, t=PACK, i=4),
-            in_=w3_raw[:].rearrange("p (b m i t) -> p b m t i", b=2, t=PACK, i=4),
-        )
-
-        v_w = [held("v_w%d" % h, HALF, U32) for h in range(2)]
-        v2_w = [[held("v2_w%d_%d" % (h, a), HALF, U32) for a in range(2)] for h in range(2)]
-        v3_w = [held("v3_w%d" % h, HALF, U16) for h in range(2)]
-
-        def gather(dst, window, idx, h):
-            cols = HALF // 16
-            nc.vector.tensor_copy(dst, window.indirect(idx[:, h * cols : (h + 1) * cols]))
-
-        w2_s = [[held("w2_s%d_%d" % (b, a), HALF, U8) for a in range(2)] for b in range(2)]
-        w4_c = [held("w4_c%d" % b, N, U32) for b in range(2)]
-        w4_s = [held("w4_s%d" % b, N, U8) for b in range(2)]
+        def round_half(grouped, raw, half):
+            m = slice(half * P // 2, (half + 1) * P // 2)
+            nc.scalar.copy(
+                out=grouped[:].rearrange("p (t m i) -> p m t i", t=PACK, i=PACK)[:, m],
+                in_=raw[:].rearrange("p i (m t) -> p m t i", t=PACK)[:, m],
+            )
 
         def round_weight(raw, tag):
             grouped = slot(tag, "w_bf", [P, PACK * HALF], BF16)
-            for m in (slice(0, P // 2), slice(P // 2, P)):
-                nc.scalar.copy(
-                    out=grouped[:].rearrange("p (t m i) -> p m t i", t=PACK, i=PACK)[:, m],
-                    in_=raw[:].rearrange("p i (m t) -> p m t i", t=PACK)[:, m],
-                )
+            for half in range(2):
+                round_half(grouped, raw, half)
             return grouped
 
         def quantise(codes, scales, grouped):
             nc.vector.quantize_mx(out=codes.bitcast(FP8X4), scales=scales, in_=grouped)
 
-        w2_raw[0, 0] = load_rows(w2, 0, 0, "A")
-        w2_raw[0, 1] = load_rows(w2, KP, 0, "B")
-        for h in range(2):
-            gather(v_w[h][:], tab_w[:].bitcast(U32), idx1, h)
-        meas_t[0, 0] = load_rows(meas, 0, 0, "C")
-        for h in range(2):
-            gather(v3_w[h][:], tab3_w[:].bitcast(U16), idx3, h)
-        meas_t[1, 0] = load_rows(meas, 0, HALF, "D")
-        for h in range(2):
-            gather(v2_w[h][0][:], tab2_w[0][:].bitcast(U32), idx2, h)
-        w2_raw[1, 0] = load_rows(w2, 0, HALF, "E")
-        for h in range(2):
-            gather(v2_w[h][1][:], tab2_w[1][:].bitcast(U32), idx2, h)
-        picked_s = slot("F", "picked_s", [P, 3 * S], U8)
-        v_s, v3_s, v2_s = [[picked_s[:, n * S + h * HALF : n * S + (h + 1) * HALF] for h in range(2)] for n in range(3)]
-        gather(v_s[0], tab_s[:], idx1, 0)
-        gather(v3_s[0], tab3_s[:], idx3, 0)
-        gather(v2_s[0], tab2_s[:], idx2, 0)
-        gather(v_s[1], tab_s[:], idx1, 1)
-        ws = slot("J", "ws", [P, 2 * H], U8)
+        tab_s = held("tab_s", T, U8)
+        tab2_s = held("tab2_s", T, U8)
+        tab3_s = slot("K", "tab3_s", [P, T3], U8)
+        ws_raw = slot("M", "ws_raw", [P, 2 * H], U8)
+        step_t = held("step_t", PACK, F32)
+        for plane in (ws_raw, tab_s, tab3_s, tab2_s):
+            nc.vector.memset(plane[:].bitcast(I32), 0)
+
+        w1_raw = load_words("A", w1_words[0].bitcast(I32))
+        w3_raw = load_words("B", words(w3_words[0]))
+        nc.sync.dma_start(idx1[:], offs)
+        tab_w = load_words("C", words(tab_words[0]))
+        nc.sync.dma_start(idx3[:], offs3)
+        tab3_w = load_words("D", tab3_words[0].bitcast(I32))
+        nc.sync.dma_start(idx2[:], offs2)
+        nc.sync.dma_start(out=step_t[:], in_=step.rearrange("(p t) -> p t", t=PACK))
+        load_scale_rows(nc.sync, tab_s, tab_scales[0])
+        load_scale_rows(nc.sync, tab3_s, tab3_scales[0])
+        load_scale_rows(nc.gpsimd, ws_raw[:, 0:H], w1_scales[0])
+        load_scale_rows(nc.gpsimd, ws_raw[:, H : 2 * H], w3_scales[0])
+        for q in range(4):
+            nc.gpsimd.dma_start(out=tab2_s[32 * q : 32 * q + 8, :].bitcast(I32), in_=tab2_scales[:, 4 * q : 4 * q + 4, :].bitcast(I32))
+
+        w1_c = held("w1_c", 2 * H, U8)
+        w3_c = held("w3_c", H, I32)
+        v_w = held("v_w", S, U32)
+        v2_w = [held("v2_w%d" % a, S, U32) for a in range(2)]
+        v3_w = held("v3_w", S, U16)
+        v_s = held("v_s", S, U8)
+        v3_s = held("v3_s", S, U8)
+        w2_c = {(b, a): held("w2_c%d%d" % (b, a), HALF, U32) for b in range(2) for a in range(2) if a + b > 0}
+        w2_raw, tab2_w = {}, {}
+        w2_s = [[held("w2_s%d%d" % (b, a), HALF, U8) for a in range(2)] for b in range(2)]
+        w4_s = [held("w4_s%d" % b, N, U8) for b in range(2)]
+
+        nc.vector.tensor_copy(
+            out=w1_c[:].bitcast(U16).rearrange("p (b t m) -> p b t m", b=2, t=PACK),
+            in_=w1_raw[:].bitcast(U16).rearrange("p (b m t) -> p b t m", b=2, t=PACK),
+        )
+        w2_raw[0, 0] = load_rows("A", w2, 0, 0)
+        nc.vector.tensor_copy(
+            out=w3_c[:].rearrange("p (b t m i) -> p b m t i", b=2, t=PACK, i=4),
+            in_=w3_raw[:].rearrange("p (b m i t) -> p b m t i", b=2, t=PACK, i=4),
+        )
+        tab2_w[0] = load_words("B", words(tab2_words[0]))
+        gather(v_w[:], tab_w[:].bitcast(U32), idx1[:])
+        w2_raw[0, 1] = load_rows("C", w2, KP, 0)
+        gather(v3_w[:], tab3_w[:].bitcast(U16), idx3[:])
+        tab2_w[1] = load_words("D", words(tab2_words[1]))
+        gather(v_s[:], tab_s[:], idx1[:])
+        w2_bf = round_weight(w2_raw[0, 0], "N")
+        w2_raw[1, 0] = load_rows("A", w2, 0, HALF)
+        gather(v2_w[0][:], tab2_w[0][:].bitcast(U32), idx2[:])
+        w2_raw[1, 1] = load_rows("B", w2, KP, HALF)
+        gather(v3_s[:], tab3_s[:], idx3[:])
+        ws = slot("K", "ws", [P, 2 * H], U8)
         nc.vector.tensor_copy(
             out=ws[:].rearrange("p (b t m) -> p b t m", b=4, t=PACK),
             in_=ws_raw[:].rearrange("p (b m t) -> p b t m", b=4, t=PACK),
         )
-        w2_c = [[slot("M", "w2_c", [P, HALF], U32)], [held("w2_c%d" % a, HALF, U32) for a in range(2)]]
-        quantise(w2_c[0][0][:], w2_s[0][0][:], round_weight(w2_raw[0, 0], "G")[:])
-        w2_raw[1, 1] = load_rows(w2, KP, HALF, "A")
-        gather(v3_s[1], tab3_s[:], idx3, 1)
-        w2_c[0].append(slot("K", "w2_c", [P, HALF], U32))
-        quantise(w2_c[0][1][:], w2_s[0][1][:], round_weight(w2_raw[0, 1], "H")[:])
-        meas_t[0, 1] = load_rows(meas, KP, 0, "B")
-        gather(v2_s[1], tab2_s[:], idx2, 1)
-        w4_raw[0] = load_rows(w4, 0, 0, "L")
+        w2_c[0, 0] = slot("M", "w2_c", [P, HALF], U32)
+        quantise(w2_c[0, 0][:], w2_s[0][0][:], w2_bf[:])
+        w2_bf = round_weight(w2_raw[0, 1], "G")
+        meas_t = [load_meas("C", 0)]
+        gather(v2_w[1][:], tab2_w[1][:].bitcast(U32), idx2[:])
+        quantise(w2_c[0, 1][:], w2_s[0][1][:], w2_bf[:])
+        meas_t.append(load_meas("G", QUARTER))
+        v2_s = slot("N", "v2_s", [P, S], U8)
+        for h in range(2):
+            gather(v2_s[:, h * HALF : (h + 1) * HALF], tab2_s[:], idx2[:, h * HALF // 16 : (h + 1) * HALF // 16])
+        quantise(w2_c[1, 0][:], w2_s[1][0][:], round_weight(w2_raw[1, 0], "step0")[:])
+        w4_raw = [load_rows("A", w4, 0, 0)]
+        quantise(w2_c[1, 1][:], w2_s[1][1][:], round_weight(w2_raw[1, 1], "step1")[:])
+        w4_raw.append(load_rows("B", w4, KP, 0))
 
-        z_c = [[held("z_c%d_%d" % (h, b), HALF, U32) for b in range(2)] for h in range(2)]
-        z_s = [[held("z_s%d_%d" % (h, b), HALF, U8) for b in range(2)] for h in range(2)]
-        y_c = held("y_c", S, U32)
+        z_s = [held("z_s%d" % c, 2 * STEP, U8) for c in range(CHUNKS)]
         y_s = held("y_s", S, U8)
-        z_bf = {}
+        z_bf, z_c, y_bf, w4_bf, w4_c, y_tiles = {}, {}, {}, {}, {}, {}
 
         def woven(bank):
-            return bank[:].rearrange("p t j -> p j t")
+            return bank.rearrange("p t j -> p j t")
 
         def as_woven(flat):
             return flat.rearrange("p (j t) -> p j t", t=PACK)
 
-        def first_products(i, h, b, c):
+        def codes_tile(i, name, width):
+            return slot("step%d" % i, name, [P, width], U32)
+
+        def make_z(i):
+            c, b = divmod(i, 2)
             cols = slice(c * STEP, (c + 1) * STEP)
+            seed = psum.tile([P, PACK, STEP], F32, name="seed", tag="seed", bufs=2)
             soil = psum.tile([P, PACK, STEP], F32, name="soil", tag="soil", bufs=2)
             rain = psum.tile([P, PACK, STEP], F32, name="rain", tag="rain", bufs=2)
-            seed = psum.tile([P, PACK, STEP], F32, name="seed", tag="seed", bufs=2)
             for t in range(PACK):
                 r0 = b * KP + t * P
                 nc.tensor.matmul_mx(
                     out=seed[:, t, :], lhsT=w1_c[:, 2 * r0 : 2 * (r0 + P)].bitcast(FP4X4), lhsT_scale=ws[:, r0 : r0 + P],
-                    rhs=v_w[h][:, cols].bitcast(FP8X4), rhs_scale=v_s[h][:, cols], start=True, stop=True,
+                    rhs=v_w[:, cols].bitcast(FP8X4), rhs_scale=v_s[:, cols], start=True, stop=True,
                 )
             for t in range(PACK):
                 wc = slice(t * P, (t + 1) * P)
                 for a in range(2):
                     nc.tensor.matmul_mx(
-                        out=soil[:, t, :], lhsT=w2_c[b][a][:, wc].bitcast(FP8X4), lhsT_scale=w2_s[b][a][:, wc],
-                        rhs=v2_w[h][a][:, cols].bitcast(FP8X4), rhs_scale=v2_s[h][4 * a : P, cols],
+                        out=soil[:, t, :], lhsT=w2_c[b, a][:, wc].bitcast(FP8X4), lhsT_scale=w2_s[b][a][:, wc],
+                        rhs=v2_w[a][:, cols].bitcast(FP8X4), rhs_scale=v2_s[4 * a : P, cols],
                         start=(a == 0), stop=(a == 1),
                     )
             for t in range(PACK):
                 r0 = b * KP + t * P
                 nc.tensor.matmul_mx(
                     out=rain[:, t, :], lhsT=w3_c[:, r0 : r0 + P].bitcast(FP8X4), lhsT_scale=ws[:, H + r0 : H + r0 + P],
-                    rhs=v3_w[h][:, cols].bitcast(FP4X4), rhs_scale=v3_s[h][:, cols], start=True, stop=True,
+                    rhs=v3_w[:, cols].bitcast(FP4X4), rhs_scale=v3_s[:, cols], start=True, stop=True,
                 )
-            square = ring.tile([P, PACK * STEP], F32, name="square", tag="square", bufs=3)
-            nc.scalar.activation(out=as_woven(square[:]), in_=woven(seed), func=SQUARE)
-            both = slot("GH"[i // 2 % 2] if i % 2 == 0 else "I", "both", [P, PACK * STEP], F32)
-            nc.vector.tensor_tensor(out=as_woven(both[:]), in0=woven(soil), in1=as_woven(square[:]), op=MULT)
+            square = slot("step%d" % i, "square", [P, PACK * STEP], F32)
+            nc.scalar.activation(out=as_woven(square[:]), in_=woven(seed[:]), func=SQUARE)
+            both = ring.tile([P, PACK * STEP], F32, name="both", tag="both", bufs=2)
+            nc.vector.tensor_tensor(out=as_woven(both[:]), in0=woven(soil[:]), in1=as_woven(square[:]), op=MULT)
             minus = ring.tile([P, PACK, STEP], F32, name="minus", tag="minus", bufs=3)
-            nc.vector.tensor_tensor(out=minus[:], in0=seed[:], in1=meas_t[h, b][:, :, cols], op=MULT)
+            q, j0 = divmod(c * STEP, QUARTER)
+            nc.vector.tensor_tensor(out=minus[:], in0=seed[:], in1=meas_t[q][:, b, :, j0 : j0 + STEP], op=MULT)
             plus = ring.tile([P, PACK * STEP], F32, name="plus", tag="plus", bufs=3)
-            nc.vector.tensor_tensor(out=as_woven(plus[:]), in0=woven(rain), in1=as_woven(both[:]), op=MULT)
-            if c == 0:
-                z_bf[h, b] = ring.tile([P, PACK * HALF], BF16, name="z_bf", tag="z_bf", bufs=2, align_bytes=64)
-            engine = nc.vector if i == len(steps) - 1 else nc.gpsimd
-            engine.tensor_tensor(
-                out=as_woven(z_bf[h, b][:, c * KP : (c + 1) * KP]), in0=as_woven(plus[:]), in1=woven(minus), op=SUB,
+            nc.vector.tensor_tensor(out=as_woven(plus[:]), in0=woven(rain[:]), in1=as_woven(both[:]), op=MULT)
+            if b == 0:
+                z_bf[c] = ring.tile([P, 2 * PACK * STEP], BF16, name="z_bf", tag="z_bf", bufs=3, align_bytes=64)
+            return lambda engine: engine.tensor_tensor(
+                out=as_woven(z_bf[c][:, b * KP : (b + 1) * KP]), in0=as_woven(plus[:]), in1=woven(minus[:]), op=SUB,
             )
 
-        def quantise_z(h, b, c0, width):
-            cols = slice(c0, c0 + width)
-            quantise(z_c[h][b][:, cols], z_s[h][b][:, cols], z_bf[h, b][:, PACK * c0 : PACK * (c0 + width)])
-
-        y_tiles = {}
         store_of = {}
         j0 = 0
-        for width in Y_CHUNKS:
+        for width in Y_STORES:
             for j in range(j0, j0 + width, STEP):
                 store_of[j] = (j0, width)
             j0 = j0 + width
 
-        def last_product(h, c):
-            cols = slice(c * STEP, (c + 1) * STEP)
-            j = h * HALF + c * STEP
+        def last_product(i, c):
+            z_c = codes_tile(i, "z_c", 2 * STEP)
+            quantise(z_c[:], z_s[c][:], z_bf[c][:])
+            return z_c
+
+        def make_y(c, z_c):
+            j = c * STEP
             j0, width = store_of[j]
             if j == j0:
                 y_tiles[j0] = ring.tile([P, PACK, width], F32, name="y", tag="y", bufs=2)
@@ -235,52 +242,63 @@ def tile_list_rice_factor_refit_kernel(
             for t in range(PACK):
                 wc = slice(t * P, (t + 1) * P)
                 for b in range(2):
+                    zc = slice(b * STEP, (b + 1) * STEP)
                     nc.tensor.matmul_mx(
                         out=bank[:, t, :], lhsT=w4_c[b][:, wc].bitcast(FP8X4), lhsT_scale=w4_s[b][:, wc],
-                        rhs=z_c[h][b][:, cols].bitcast(FP8X4), rhs_scale=z_s[h][b][:, cols],
+                        rhs=z_c[:, zc].bitcast(FP8X4), rhs_scale=z_s[c][:, zc],
                         start=(b == 0), stop=(b == 1),
                     )
-            for t in range(PACK):
-                nc.scalar.activation(out=y[:, t, :], in_=bank[:, t, :], func=COPY, scale=step_t[:, t : t + 1])
+            y_bf[c] = ring.tile([P, PACK * STEP], BF16, name="y_bf", tag="y_bf", bufs=3, align_bytes=64)
+            if c == CHUNKS - 1:
+                nc.vector.tensor_tensor(out=y, in0=bank[:], in1=step_t[:].unsqueeze(2).to_broadcast([P, PACK, STEP]), op=MULT)
+            else:
+                for t in range(PACK):
+                    nc.scalar.activation(out=y[:, t, :], in_=bank[:, t, :], func=COPY, scale=step_t[:, t : t + 1])
             if j + STEP == j0 + width:
                 nc.sync.dma_start(out=out_0[:, j0 : j0 + width].rearrange("(p t) j -> p t j", t=PACK), in_=y_tiles[j0][:])
-            y_bf = ring.tile([P, PACK * STEP], BF16, name="y_bf", tag="y_bf", bufs=2, align_bytes=64)
-            if j + 2 * STEP >= S:
-                nc.vector.tensor_copy(out=as_woven(y_bf[:]), in_=y.rearrange("p t j -> p j t"))
+            return y
+
+        def round_y(c, y):
+            if c == CHUNKS - 1:
+                nc.vector.tensor_copy(out=as_woven(y_bf[c][:]), in_=woven(y))
             else:
-                nc.scalar.copy(out=as_woven(y_bf[:]), in_=y.rearrange("p t j -> p j t"))
-            return j, y_bf
+                nc.scalar.copy(out=as_woven(y_bf[c][:]), in_=woven(y))
 
-        def planes(j, y_bf):
-            quantise(y_c[:, j : j + STEP], y_s[:, j : j + STEP], y_bf[:])
-            j0, width = store_of[j]
-            if j + STEP == j0 + width:
-                nc.sync.dma_start(out=words(out_1[0])[:, j0 : j0 + width], in_=y_c[:, j0 : j0 + width].bitcast(I32))
+        def planes(i, c):
+            cols = slice(c * STEP, (c + 1) * STEP)
+            y_c = codes_tile(i, "y_c", STEP)
+            quantise(y_c[:], y_s[:, cols], y_bf[c][:])
+            nc.sync.dma_start(out=words(out_1[0])[:, cols], in_=y_c[:].bitcast(I32))
 
-        steps = [(h, b, c) for b in range(2) for h in range(2) for c in range(HALF // STEP)]
-        rounded = {}
-        for i in range(len(steps) + LAG + 2):
-            if i < len(steps):
-                first_products(i, *steps[i])
-            if i in (0, 2):
-                a = i // 2
-                quantise(w2_c[1][a][:], w2_s[1][a][:], round_weight(w2_raw[1, a], "GH"[a])[:])
-            if i == 0:
-                w4_raw[1] = load_rows(w4, KP, 0, "E")
-            if i == 2:
-                meas_t[1, 1] = load_rows(meas, KP, HALF, "A")
-            if i in (4, 6):
-                a = i // 2 - 2
-                quantise(w4_c[a][:], w4_s[a][:], round_weight(w4_raw[a], "GH"[a])[:])
-            n = i - LAG
-            if n - 2 in rounded:
-                planes(*rounded[n - 2])
-            if 1 <= n <= len(steps):
-                h, b, c = steps[n - 1]
-                if b == 0 and c == HALF // STEP - 1:
-                    quantise_z(h, 0, 0, HALF)
-                if b == 1:
-                    quantise_z(h, 1, c * STEP, STEP)
-                    rounded[n - 1] = last_product(h, c)
+        last = 2 * CHUNKS - 1
+        for i in range(2 * CHUNKS):
+            subtract = make_z(i)
+            if i < last:
+                subtract(nc.gpsimd)
+            if i < 4:
+                b, half = divmod(i, 2)
+                if half == 0:
+                    w4_bf[b] = slot("step%d" % b, "w_bf", [P, PACK * HALF], BF16)
+                round_half(w4_bf[b], w4_raw[b], half)
+                if half == 1:
+                    meas_t.append(load_meas("AB"[b], (2 + b) * QUARTER))
+            if i in (2, 4):
+                b = i // 2 - 1
+                w4_c[b] = codes_tile(i, "w4_c", N)
+                quantise(w4_c[b][:], w4_s[b][:], w4_bf[b][:])
+            if i % 2 == 1 and i >= 3:
+                z_c[i // 2 - 1] = last_product(i, i // 2 - 1)
+            if i == 4:
+                round_y(0, make_y(0, z_c[0]))
+            if i % 2 == 1 and i >= 5:
+                round_y(i // 2 - 1, make_y(i // 2 - 1, z_c[i // 2 - 1]))
+            if i % 2 == 0 and i >= 6:
+                planes(i, i // 2 - 3)
+        subtract(nc.vector)
+        planes(last + 1, CHUNKS - 3)
+        y = make_y(CHUNKS - 1, last_product(last + 2, CHUNKS - 1))
+        planes(last + 3, CHUNKS - 2)
+        round_y(CHUNKS - 1, y)
+        planes(last + 4, CHUNKS - 1)
         for q in range(4):
             nc.sync.dma_start(out=out_2[0, 4 * q : 4 * q + 4, :].bitcast(I32), in_=y_s[32 * q : 32 * q + 4, :].bitcast(I32))

@@ -173,6 +173,9 @@ def tile_list_rice_factor_refit_kernel(
         def woven(bank):
             return bank.rearrange("p t j -> p j t")
 
+        def paired(rows):
+            return rows.rearrange("p (u e) j -> p u j e", e=2)
+
         def as_woven(flat):
             return flat.rearrange("p (j t) -> p j t", t=PACK)
 
@@ -209,15 +212,17 @@ def tile_list_rice_factor_refit_kernel(
             nc.scalar.activation(out=as_woven(square[:]), in_=woven(seed[:]), func=SQUARE)
             both = ring.tile([P, PACK * STEP], F32, name="both", tag="both", bufs=2)
             nc.vector.tensor_tensor(out=as_woven(both[:]), in0=woven(soil[:]), in1=as_woven(square[:]), op=MULT)
-            minus = ring.tile([P, PACK, STEP], F32, name="minus", tag="minus", bufs=3)
+            minus = ring.tile([P, 2, STEP, 2], F32, name="minus", tag="minus", bufs=3)
             q, j0 = divmod(c * STEP, QUARTER)
-            nc.vector.tensor_tensor(out=minus[:], in0=seed[:], in1=meas_t[q][:, b, :, j0 : j0 + STEP], op=MULT)
+            nc.vector.tensor_tensor(out=minus[:], in0=paired(seed[:]), in1=paired(meas_t[q][:, b, :, j0 : j0 + STEP]), op=MULT)
             plus = ring.tile([P, PACK * STEP], F32, name="plus", tag="plus", bufs=3)
             nc.vector.tensor_tensor(out=as_woven(plus[:]), in0=woven(rain[:]), in1=as_woven(both[:]), op=MULT)
             if b == 0:
                 z_bf[c] = ring.tile([P, 2 * PACK * STEP], BF16, name="z_bf", tag="z_bf", bufs=3, align_bytes=64)
             return lambda engine: engine.tensor_tensor(
-                out=as_woven(z_bf[c][:, b * KP : (b + 1) * KP]), in0=as_woven(plus[:]), in1=woven(minus[:]), op=SUB,
+                out=z_bf[c][:, b * KP : (b + 1) * KP].rearrange("p (j u e) -> p j u e", u=2, e=2),
+                in0=plus[:].rearrange("p (j u e) -> p j u e", u=2, e=2),
+                in1=minus[:].rearrange("p u j e -> p j u e"), op=SUB,
             )
 
         store_of = {}
@@ -301,4 +306,5 @@ def tile_list_rice_factor_refit_kernel(
         round_y(CHUNKS - 1, y)
         planes(last + 4, CHUNKS - 1)
         for q in range(4):
-            nc.sync.dma_start(out=out_2[0, 4 * q : 4 * q + 4, :].bitcast(I32), in_=y_s[32 * q : 32 * q + 4, :].bitcast(I32))
+            queue = nc.scalar if q % 2 else nc.sync
+            queue.dma_start(out=out_2[0, 4 * q : 4 * q + 4, :].bitcast(I32), in_=y_s[32 * q : 32 * q + 4, :].bitcast(I32))

@@ -20,11 +20,12 @@ COPY = mybir.ActivationFunctionType.Copy
 
 P = 128
 PACK = 4
-KP = P * PACK
-HALF = 512
-STEP = 128
-QUARTER = 256
-CHUNKS = S // STEP
+PASS = P * PACK
+LINE = 4
+CHUNK = 128
+CHUNKS = S // CHUNK
+STEPS = 2 * CHUNKS
+MEAS_COLS = 256
 Y_STORES = (256, 256, 256, 128, 128)
 
 
@@ -35,7 +36,7 @@ def tile_list_rice_factor_refit_kernel(
     nc = tc.nc
     with ExitStack() as ctx:
         keep = ctx.enter_context(tc.tile_pool(name="keep", bufs=1))
-        ring = ctx.enter_context(tc.tile_pool(name="ring", bufs=2))
+        shared = ctx.enter_context(tc.tile_pool(name="shared", bufs=2))
         psum = ctx.enter_context(tc.psum_pool(name="psum", bufs=1))
 
         def held(name, width, dtype):
@@ -45,26 +46,30 @@ def tile_list_rice_factor_refit_kernel(
         idx2 = keep.tile([P, S // 16], U16, name="idx2")
         idx3 = keep.tile([P, S // 16], U16, name="idx3")
 
-        def slot(tag, name, shape, dtype):
-            return ring.tile(shape, dtype, name=name, tag=tag, bufs=1, align_bytes=64)
+        def tenant(tag, name, shape, dtype):
+            return shared.tile(shape, dtype, name=name, tag=tag, bufs=1, align_bytes=64)
+
+        def step_tag(i):
+            return "step%d" % i
 
         def words(ap):
             return ap.rearrange("p n t -> p (n t)").bitcast(I32)
 
         def load_words(tag, src):
-            raw = slot(tag, "packed", [P, src.shape[1]], I32)
+            raw = tenant(tag, "packed", [P, src.shape[1]], I32)
             nc.sync.dma_start(out=raw[:], in_=src)
             return raw
 
-        def load_rows(tag, src, row0, col0):
-            raw = slot(tag, "rows", [P, PACK, HALF], F32)
-            nc.sync.dma_start(out=raw[:], in_=src[row0 : row0 + KP, col0 : col0 + HALF].rearrange("(p i) c -> p i c", i=PACK))
+        def load_weight(tag, src, a, b):
+            raw = tenant(tag, "weight", [P, PACK, PASS], F32)
+            rows = src[a * PASS : (a + 1) * PASS, b * PASS : (b + 1) * PASS]
+            nc.sync.dma_start(out=raw[:], in_=rows.rearrange("(p i) c -> p i c", i=PACK))
             return raw
 
-        def load_meas(tag, col0):
-            raw = slot(tag, "meas_t", [P, 2, PACK, QUARTER], F32)
+        def load_meas(tag, q):
+            raw = tenant(tag, "meas_t", [P, 2, PACK, MEAS_COLS], F32)
             for b in range(2):
-                rows = meas[b * KP : (b + 1) * KP, col0 : col0 + QUARTER]
+                rows = meas[b * PASS : (b + 1) * PASS, q * MEAS_COLS : (q + 1) * MEAS_COLS]
                 nc.sync.dma_start(out=raw[:, b], in_=rows.rearrange("(p t) j -> p t j", t=PACK))
             return raw
 
@@ -78,12 +83,12 @@ def tile_list_rice_factor_refit_kernel(
         def round_half(grouped, raw, half):
             m = slice(half * P // 2, (half + 1) * P // 2)
             nc.scalar.copy(
-                out=grouped[:].rearrange("p (t m i) -> p m t i", t=PACK, i=PACK)[:, m],
-                in_=raw[:].rearrange("p i (m t) -> p m t i", t=PACK)[:, m],
+                out=grouped[:].rearrange("p (t m i) -> p m i t", t=PACK, i=PACK)[:, m],
+                in_=raw[:].rearrange("p i (m t) -> p m i t", t=PACK)[:, m],
             )
 
         def round_weight(raw, tag):
-            grouped = slot(tag, "w_bf", [P, PACK * HALF], BF16)
+            grouped = tenant(tag, "w_bf", [P, PACK * PASS], BF16)
             for half in range(2):
                 round_half(grouped, raw, half)
             return grouped
@@ -93,10 +98,10 @@ def tile_list_rice_factor_refit_kernel(
 
         tab_s = held("tab_s", T, U8)
         tab2_s = held("tab2_s", T, U8)
-        tab3_s = slot("K", "tab3_s", [P, T3], U8)
-        ws_raw = slot("M", "ws_raw", [P, 2 * H], U8)
+        tab3_s = tenant("K", "tab3_s", [P, T3], U8)
+        w13_s_raw = tenant("M", "w13_s_raw", [P, 2 * H], U8)
         step_t = held("step_t", PACK, F32)
-        for plane in (ws_raw, tab_s, tab3_s, tab2_s):
+        for plane in (w13_s_raw, tab_s, tab3_s, tab2_s):
             nc.vector.memset(plane[:].bitcast(I32), 0)
 
         w1_raw = load_words("A", w1_words[0].bitcast(I32))
@@ -109,8 +114,8 @@ def tile_list_rice_factor_refit_kernel(
         nc.sync.dma_start(out=step_t[:], in_=step.rearrange("(p t) -> p t", t=PACK))
         load_scale_rows(nc.sync, tab_s, tab_scales[0])
         load_scale_rows(nc.sync, tab3_s, tab3_scales[0])
-        load_scale_rows(nc.gpsimd, ws_raw[:, 0:H], w1_scales[0])
-        load_scale_rows(nc.gpsimd, ws_raw[:, H : 2 * H], w3_scales[0])
+        load_scale_rows(nc.gpsimd, w13_s_raw[:, 0:H], w1_scales[0])
+        load_scale_rows(nc.gpsimd, w13_s_raw[:, H : 2 * H], w3_scales[0])
         for q in range(4):
             nc.gpsimd.dma_start(out=tab2_s[32 * q : 32 * q + 8, :].bitcast(I32), in_=tab2_scales[:, 4 * q : 4 * q + 4, :].bitcast(I32))
 
@@ -121,77 +126,77 @@ def tile_list_rice_factor_refit_kernel(
         v3_w = held("v3_w", S, U16)
         v_s = held("v_s", S, U8)
         v3_s = held("v3_s", S, U8)
-        w2_c = {(b, a): held("w2_c%d%d" % (b, a), HALF, U32) for b in range(2) for a in range(2) if a + b > 0}
-        w2_raw, tab2_w = {}, {}
-        w2_s = [[held("w2_s%d%d" % (b, a), HALF, U8) for a in range(2)] for b in range(2)]
+        w2_c = {(b, a): held("w2_c%d%d" % (b, a), PASS, U32) for b in range(2) for a in range(2) if a + b > 0}
+        w2_s = [[held("w2_s%d%d" % (b, a), PASS, U8) for a in range(2)] for b in range(2)]
         w4_s = [held("w4_s%d" % b, N, U8) for b in range(2)]
+        w2_raw, tab2_w, w4_raw, meas_t = {}, {}, {}, {}
 
         nc.vector.tensor_copy(
             out=w1_c[:].bitcast(U16).rearrange("p (b t m) -> p b t m", b=2, t=PACK),
             in_=w1_raw[:].bitcast(U16).rearrange("p (b m t) -> p b t m", b=2, t=PACK),
         )
-        w2_raw[0, 0] = load_rows("A", w2, 0, 0)
+        w2_raw[0, 0] = load_weight("A", w2, 0, 0)
         nc.vector.tensor_copy(
-            out=w3_c[:].rearrange("p (b t m i) -> p b m t i", b=2, t=PACK, i=4),
-            in_=w3_raw[:].rearrange("p (b m i t) -> p b m t i", b=2, t=PACK, i=4),
+            out=w3_c[:].rearrange("p (b t m i) -> p b m t i", b=2, t=PACK, i=LINE),
+            in_=w3_raw[:].rearrange("p (b m i t) -> p b m t i", b=2, t=PACK, i=LINE),
         )
         tab2_w[0] = load_words("B", words(tab2_words[0]))
         gather(v_w[:], tab_w[:].bitcast(U32), idx1[:])
-        w2_raw[0, 1] = load_rows("C", w2, KP, 0)
+        w2_raw[0, 1] = load_weight("C", w2, 1, 0)
         gather(v3_w[:], tab3_w[:].bitcast(U16), idx3[:])
         tab2_w[1] = load_words("D", words(tab2_words[1]))
         gather(v_s[:], tab_s[:], idx1[:])
         w2_bf = round_weight(w2_raw[0, 0], "N")
-        w2_raw[1, 0] = load_rows("A", w2, 0, HALF)
+        w2_raw[1, 0] = load_weight("A", w2, 0, 1)
         gather(v2_w[0][:], tab2_w[0][:].bitcast(U32), idx2[:])
-        w2_raw[1, 1] = load_rows("B", w2, KP, HALF)
+        w2_raw[1, 1] = load_weight("B", w2, 1, 1)
         gather(v3_s[:], tab3_s[:], idx3[:])
-        ws = slot("K", "ws", [P, 2 * H], U8)
+        w13_s = tenant("K", "w13_s", [P, 2 * H], U8)
         nc.vector.tensor_copy(
-            out=ws[:].rearrange("p (b t m) -> p b t m", b=4, t=PACK),
-            in_=ws_raw[:].rearrange("p (b m t) -> p b t m", b=4, t=PACK),
+            out=w13_s[:].rearrange("p (g t m) -> p g t m", g=2 * H // PASS, t=PACK),
+            in_=w13_s_raw[:].rearrange("p (g m t) -> p g t m", g=2 * H // PASS, t=PACK),
         )
-        w2_c[0, 0] = slot("M", "w2_c", [P, HALF], U32)
+        w2_c[0, 0] = tenant("M", "w2_c", [P, PASS], U32)
         quantise(w2_c[0, 0][:], w2_s[0][0][:], w2_bf[:])
         w2_bf = round_weight(w2_raw[0, 1], "G")
-        meas_t = [load_meas("C", 0)]
+        meas_t[0] = load_meas("C", 0)
         gather(v2_w[1][:], tab2_w[1][:].bitcast(U32), idx2[:])
         quantise(w2_c[0, 1][:], w2_s[0][1][:], w2_bf[:])
-        meas_t.append(load_meas("G", QUARTER))
-        v2_s = slot("N", "v2_s", [P, S], U8)
+        w4_raw[0] = load_weight("G", w4, 0, 0)
+        v2_s = tenant("N", "v2_s", [P, S], U8)
         for h in range(2):
-            gather(v2_s[:, h * HALF : (h + 1) * HALF], tab2_s[:], idx2[:, h * HALF // 16 : (h + 1) * HALF // 16])
-        quantise(w2_c[1, 0][:], w2_s[1][0][:], round_weight(w2_raw[1, 0], "step0")[:])
-        w4_raw = [load_rows("A", w4, 0, 0)]
-        quantise(w2_c[1, 1][:], w2_s[1][1][:], round_weight(w2_raw[1, 1], "step1")[:])
-        w4_raw.append(load_rows("B", w4, KP, 0))
+            gather(v2_s[:, h * S // 2 : (h + 1) * S // 2], tab2_s[:], idx2[:, h * S // 32 : (h + 1) * S // 32])
+        quantise(w2_c[1, 0][:], w2_s[1][0][:], round_weight(w2_raw[1, 0], step_tag(0))[:])
+        meas_t[1] = load_meas("A", 1)
+        quantise(w2_c[1, 1][:], w2_s[1][1][:], round_weight(w2_raw[1, 1], step_tag(1))[:])
+        w4_raw[1] = load_weight("B", w4, 1, 0)
 
-        z_s = [held("z_s%d" % c, 2 * STEP, U8) for c in range(CHUNKS)]
+        z_s = [held("z_s%d" % c, 2 * CHUNK, U8) for c in range(CHUNKS)]
         y_s = held("y_s", S, U8)
         z_bf, z_c, y_bf, w4_bf, w4_c, y_tiles = {}, {}, {}, {}, {}, {}
 
-        def woven(bank):
-            return bank.rearrange("p t j -> p j t")
-
-        def paired(rows):
-            return rows.rearrange("p (u e) j -> p u j e", e=2)
+        def woven(rows):
+            return rows.rearrange("p t j -> p j t")
 
         def as_woven(flat):
             return flat.rearrange("p (j t) -> p j t", t=PACK)
 
-        def codes_tile(i, name, width):
-            return slot("step%d" % i, name, [P, width], U32)
+        def paired(rows):
+            return rows.rearrange("p (u e) j -> p u j e", e=2)
 
-        def make_z(i):
+        def codes_tile(i, name, width):
+            return tenant(step_tag(i), name, [P, width], U32)
+
+        def products(i):
             c, b = divmod(i, 2)
-            cols = slice(c * STEP, (c + 1) * STEP)
-            seed = psum.tile([P, PACK, STEP], F32, name="seed", tag="seed", bufs=2)
-            soil = psum.tile([P, PACK, STEP], F32, name="soil", tag="soil", bufs=2)
-            rain = psum.tile([P, PACK, STEP], F32, name="rain", tag="rain", bufs=2)
+            cols = slice(c * CHUNK, (c + 1) * CHUNK)
+            seed = psum.tile([P, PACK, CHUNK], F32, name="seed", tag="seed", bufs=2)
+            soil = psum.tile([P, PACK, CHUNK], F32, name="soil", tag="soil", bufs=2)
+            rain = psum.tile([P, PACK, CHUNK], F32, name="rain", tag="rain", bufs=2)
             for t in range(PACK):
-                r0 = b * KP + t * P
+                r0 = b * PASS + t * P
                 nc.tensor.matmul_mx(
-                    out=seed[:, t, :], lhsT=w1_c[:, 2 * r0 : 2 * (r0 + P)].bitcast(FP4X4), lhsT_scale=ws[:, r0 : r0 + P],
+                    out=seed[:, t, :], lhsT=w1_c[:, 2 * r0 : 2 * (r0 + P)].bitcast(FP4X4), lhsT_scale=w13_s[:, r0 : r0 + P],
                     rhs=v_w[:, cols].bitcast(FP8X4), rhs_scale=v_s[:, cols], start=True, stop=True,
                 )
             for t in range(PACK):
@@ -203,108 +208,108 @@ def tile_list_rice_factor_refit_kernel(
                         start=(a == 0), stop=(a == 1),
                     )
             for t in range(PACK):
-                r0 = b * KP + t * P
+                r0 = b * PASS + t * P
                 nc.tensor.matmul_mx(
-                    out=rain[:, t, :], lhsT=w3_c[:, r0 : r0 + P].bitcast(FP8X4), lhsT_scale=ws[:, H + r0 : H + r0 + P],
+                    out=rain[:, t, :], lhsT=w3_c[:, r0 : r0 + P].bitcast(FP8X4), lhsT_scale=w13_s[:, H + r0 : H + r0 + P],
                     rhs=v3_w[:, cols].bitcast(FP4X4), rhs_scale=v3_s[:, cols], start=True, stop=True,
                 )
-            square = slot("step%d" % i, "square", [P, PACK * STEP], F32)
+            square = tenant(step_tag(i), "square", [P, PACK * CHUNK], F32)
             nc.scalar.activation(out=as_woven(square[:]), in_=woven(seed[:]), func=SQUARE)
-            both = ring.tile([P, PACK * STEP], F32, name="both", tag="both", bufs=2)
-            nc.vector.tensor_tensor(out=as_woven(both[:]), in0=woven(soil[:]), in1=as_woven(square[:]), op=MULT)
-            minus = ring.tile([P, 2, STEP, 2], F32, name="minus", tag="minus", bufs=3)
-            q, j0 = divmod(c * STEP, QUARTER)
-            nc.vector.tensor_tensor(out=minus[:], in0=paired(seed[:]), in1=paired(meas_t[q][:, b, :, j0 : j0 + STEP]), op=MULT)
-            plus = ring.tile([P, PACK * STEP], F32, name="plus", tag="plus", bufs=3)
-            nc.vector.tensor_tensor(out=as_woven(plus[:]), in0=woven(rain[:]), in1=as_woven(both[:]), op=MULT)
+            partial = shared.tile([P, PACK * CHUNK], F32, name="partial", tag="partial", bufs=2)
+            nc.vector.tensor_tensor(out=as_woven(partial[:]), in0=woven(soil[:]), in1=as_woven(square[:]), op=MULT)
+            minus = shared.tile([P, 2, CHUNK, 2], F32, name="minus", tag="minus", bufs=3)
+            q, col = divmod(c * CHUNK, MEAS_COLS)
+            nc.vector.tensor_tensor(out=minus[:], in0=paired(seed[:]), in1=paired(meas_t[q][:, b, :, col : col + CHUNK]), op=MULT)
+            plus = shared.tile([P, PACK * CHUNK], F32, name="plus", tag="plus", bufs=3)
+            nc.vector.tensor_tensor(out=as_woven(plus[:]), in0=woven(rain[:]), in1=as_woven(partial[:]), op=MULT)
             if b == 0:
-                z_bf[c] = ring.tile([P, 2 * PACK * STEP], BF16, name="z_bf", tag="z_bf", bufs=3, align_bytes=64)
+                z_bf[c] = shared.tile([P, 2 * PASS], BF16, name="z_bf", tag="z_bf", bufs=3, align_bytes=64)
             return lambda engine: engine.tensor_tensor(
-                out=z_bf[c][:, b * KP : (b + 1) * KP].rearrange("p (j u e) -> p j u e", u=2, e=2),
+                out=z_bf[c][:, b * PASS : (b + 1) * PASS].rearrange("p (j u e) -> p j u e", u=2, e=2),
                 in0=plus[:].rearrange("p (j u e) -> p j u e", u=2, e=2),
                 in1=minus[:].rearrange("p u j e -> p j u e"), op=SUB,
             )
 
         store_of = {}
-        j0 = 0
-        for width in Y_STORES:
-            for j in range(j0, j0 + width, STEP):
-                store_of[j] = (j0, width)
-            j0 = j0 + width
+        for n, width in enumerate(Y_STORES):
+            first = sum(Y_STORES[:n])
+            for j in range(first, first + width, CHUNK):
+                store_of[j] = (first, width)
 
-        def last_product(i, c):
-            z_c = codes_tile(i, "z_c", 2 * STEP)
-            quantise(z_c[:], z_s[c][:], z_bf[c][:])
-            return z_c
+        def quantise_z(i, c):
+            z_c[c] = codes_tile(i, "z_c", 2 * CHUNK)
+            quantise(z_c[c][:], z_s[c][:], z_bf[c][:])
 
-        def make_y(c, z_c):
-            j = c * STEP
-            j0, width = store_of[j]
-            if j == j0:
-                y_tiles[j0] = ring.tile([P, PACK, width], F32, name="y", tag="y", bufs=2)
-            y = y_tiles[j0][:, :, j - j0 : j - j0 + STEP]
-            bank = psum.tile([P, PACK, STEP], F32, name="y_bank", tag="y_bank", bufs=2)
+        def make_y(c):
+            j = c * CHUNK
+            first, width = store_of[j]
+            if j == first:
+                y_tiles[first] = shared.tile([P, PACK, width], F32, name="y", tag="y", bufs=2)
+            y = y_tiles[first][:, :, j - first : j - first + CHUNK]
+            bank = psum.tile([P, PACK, CHUNK], F32, name="y_bank", tag="y_bank", bufs=2)
             for t in range(PACK):
                 wc = slice(t * P, (t + 1) * P)
                 for b in range(2):
-                    zc = slice(b * STEP, (b + 1) * STEP)
+                    zc = slice(b * CHUNK, (b + 1) * CHUNK)
                     nc.tensor.matmul_mx(
                         out=bank[:, t, :], lhsT=w4_c[b][:, wc].bitcast(FP8X4), lhsT_scale=w4_s[b][:, wc],
-                        rhs=z_c[:, zc].bitcast(FP8X4), rhs_scale=z_s[c][:, zc],
+                        rhs=z_c[c][:, zc].bitcast(FP8X4), rhs_scale=z_s[c][:, zc],
                         start=(b == 0), stop=(b == 1),
                     )
-            y_bf[c] = ring.tile([P, PACK * STEP], BF16, name="y_bf", tag="y_bf", bufs=3, align_bytes=64)
+            y_bf[c] = shared.tile([P, PACK * CHUNK], BF16, name="y_bf", tag="y_bf", bufs=3, align_bytes=64)
             if c == CHUNKS - 1:
-                nc.vector.tensor_tensor(out=y, in0=bank[:], in1=step_t[:].unsqueeze(2).to_broadcast([P, PACK, STEP]), op=MULT)
+                nc.vector.tensor_tensor(out=y, in0=bank[:], in1=step_t[:].unsqueeze(2).to_broadcast([P, PACK, CHUNK]), op=MULT)
             else:
                 for t in range(PACK):
                     nc.scalar.activation(out=y[:, t, :], in_=bank[:, t, :], func=COPY, scale=step_t[:, t : t + 1])
-            if j + STEP == j0 + width:
-                nc.sync.dma_start(out=out_0[:, j0 : j0 + width].rearrange("(p t) j -> p t j", t=PACK), in_=y_tiles[j0][:])
+            if j + CHUNK == first + width:
+                nc.sync.dma_start(out=out_0[:, first : first + width].rearrange("(p t) j -> p t j", t=PACK), in_=y_tiles[first][:])
             return y
 
         def round_y(c, y):
+            dst = y_bf[c][:].rearrange("p (g i t) -> p g t i", i=LINE, t=PACK)
+            src = y.rearrange("p t (g i) -> p g t i", i=LINE)
             if c == CHUNKS - 1:
-                nc.vector.tensor_copy(out=as_woven(y_bf[c][:]), in_=woven(y))
+                nc.vector.tensor_copy(out=dst, in_=src)
             else:
-                nc.scalar.copy(out=as_woven(y_bf[c][:]), in_=woven(y))
+                nc.scalar.copy(out=dst, in_=src)
 
-        def planes(i, c):
-            cols = slice(c * STEP, (c + 1) * STEP)
-            y_c = codes_tile(i, "y_c", STEP)
+        def quantise_y(i, c):
+            cols = slice(c * CHUNK, (c + 1) * CHUNK)
+            y_c = codes_tile(i, "y_c", CHUNK)
             quantise(y_c[:], y_s[:, cols], y_bf[c][:])
             nc.sync.dma_start(out=words(out_1[0])[:, cols], in_=y_c[:].bitcast(I32))
 
-        last = 2 * CHUNKS - 1
-        for i in range(2 * CHUNKS):
-            subtract = make_z(i)
-            if i < last:
+        for i in range(STEPS):
+            c, b = divmod(i, 2)
+            subtract = products(i)
+            if i < STEPS - 1:
                 subtract(nc.gpsimd)
-            if i < 4:
-                b, half = divmod(i, 2)
-                if half == 0:
-                    w4_bf[b] = slot("step%d" % b, "w_bf", [P, PACK * HALF], BF16)
-                round_half(w4_bf[b], w4_raw[b], half)
-                if half == 1:
-                    meas_t.append(load_meas("AB"[b], (2 + b) * QUARTER))
-            if i in (2, 4):
-                b = i // 2 - 1
-                w4_c[b] = codes_tile(i, "w4_c", N)
-                quantise(w4_c[b][:], w4_s[b][:], w4_bf[b][:])
-            if i % 2 == 1 and i >= 3:
-                z_c[i // 2 - 1] = last_product(i, i // 2 - 1)
-            if i == 4:
-                round_y(0, make_y(0, z_c[0]))
-            if i % 2 == 1 and i >= 5:
-                round_y(i // 2 - 1, make_y(i // 2 - 1, z_c[i // 2 - 1]))
-            if i % 2 == 0 and i >= 6:
-                planes(i, i // 2 - 3)
+            if c < 2:
+                if b == 0:
+                    w4_bf[c] = tenant(step_tag(c), "w_bf", [P, PACK * PASS], BF16)
+                round_half(w4_bf[c], w4_raw[c], b)
+                if b == 1:
+                    meas_t[2 + c] = load_meas("GB"[c], 2 + c)
+            if b == 0 and c - 1 in w4_bf:
+                w4_c[c - 1] = codes_tile(i, "w4_c", N)
+                quantise(w4_c[c - 1][:], w4_s[c - 1][:], w4_bf[c - 1][:])
+            if b == 1 and c >= 1:
+                quantise_z(i, c - 1)
+            if (c, b) == (2, 0):
+                round_y(0, make_y(0))
+            if b == 1 and c >= 2:
+                round_y(c - 1, make_y(c - 1))
+            if b == 0 and c >= 3:
+                quantise_y(i, c - 3)
+
         subtract(nc.vector)
-        planes(last + 1, CHUNKS - 3)
-        y = make_y(CHUNKS - 1, last_product(last + 2, CHUNKS - 1))
-        planes(last + 3, CHUNKS - 2)
-        round_y(CHUNKS - 1, y)
-        planes(last + 4, CHUNKS - 1)
+        quantise_y(STEPS, CHUNKS - 3)
+        quantise_z(STEPS + 1, CHUNKS - 1)
+        y_last = make_y(CHUNKS - 1)
+        quantise_y(STEPS + 2, CHUNKS - 2)
+        round_y(CHUNKS - 1, y_last)
+        quantise_y(STEPS + 3, CHUNKS - 1)
         for q in range(4):
             queue = nc.scalar if q % 2 else nc.sync
             queue.dma_start(out=out_2[0, 4 * q : 4 * q + 4, :].bitcast(I32), in_=y_s[32 * q : 32 * q + 4, :].bitcast(I32))

from contextlib import ExitStack

import concourse.mybir as mybir

K, K2, H, N, T, T3, S = 512, 1024, 1024, 512, 2048, 4096, 1024
FLOPS = 2 * S * (K * H + K2 * H + K * H + H * N)

F32 = mybir.dt.float32
BF16 = mybir.dt.bfloat16
I32 = mybir.dt.int32
U32 = mybir.dt.uint32
U16 = mybir.dt.uint16
U8 = mybir.dt.uint8
FP8X4 = mybir.dt.float8_e4m3fn_x4
FP4X4 = mybir.dt.float4_e2m1fn_x4
MULT = mybir.AluOpType.mult
SUB = mybir.AluOpType.subtract
SQUARE = mybir.ActivationFunctionType.Square
COPY = mybir.ActivationFunctionType.Copy

P = 128
PACK = 4
PASS = P * PACK
LINE = 4
CHUNK = 128
CHUNKS = S // CHUNK
STEPS = 2 * CHUNKS
MEAS_COLS = 256
Y_STORES = (256, 256, 256, 128, 128)


def tile_list_rice_factor_refit_kernel(
    tc, tab_words, tab_scales, tab2_words, tab2_scales, tab3_words, tab3_scales, offs, offs2, offs3,
    w1_words, w1_scales, w2, w3_words, w3_scales, meas, w4, step, out_0, out_1, out_2,
):
    nc = tc.nc
    with ExitStack() as ctx:
        keep = ctx.enter_context(tc.tile_pool(name="keep", bufs=1))
        shared = ctx.enter_context(tc.tile_pool(name="shared", bufs=2))
        psum = ctx.enter_context(tc.psum_pool(name="psum", bufs=1))

        def held(name, width, dtype):
            return keep.tile([P, width], dtype, name=name, align_bytes=64)

        idx1 = keep.tile([P, S // 16], U16, name="idx1")
        idx2 = keep.tile([P, S // 16], U16, name="idx2")
        idx3 = keep.tile([P, S // 16], U16, name="idx3")

        def tenant(tag, name, shape, dtype):
            return shared.tile(shape, dtype, name=name, tag=tag, bufs=1, align_bytes=64)

        def step_tag(i):
            return "step%d" % i

        def words(ap):
            return ap.rearrange("p n t -> p (n t)").bitcast(I32)

        def load_words(tag, src):
            raw = tenant(tag, "packed", [P, src.shape[1]], I32)
            nc.sync.dma_start(out=raw[:], in_=src)
            return raw

        def load_weight(tag, src, a, b):
            raw = tenant(tag, "weight", [P, PACK, PASS], F32)
            rows = src[a * PASS : (a + 1) * PASS, b * PASS : (b + 1) * PASS]
            nc.sync.dma_start(out=raw[:], in_=rows.rearrange("(p i) c -> p i c", i=PACK))
            return raw

        def load_meas(tag, q):
            raw = tenant(tag, "meas_t", [P, 2, PACK, MEAS_COLS], F32)
            for b in range(2):
                rows = meas[b * PASS : (b + 1) * PASS, q * MEAS_COLS : (q + 1) * MEAS_COLS]
                nc.sync.dma_start(out=raw[:, b], in_=rows.rearrange("(p t) j -> p t j", t=PACK))
            return raw

        def load_scale_rows(queue, plane, rows):
            for q in range(4):
                queue.dma_start(out=plane[32 * q : 32 * q + 4, :].bitcast(I32), in_=rows[4 * q : 4 * q + 4, :].bitcast(I32))

        def gather(dst, window, idx):
            nc.vector.tensor_copy(dst, window.indirect(idx))

        def round_half(grouped, raw, half):
            m = slice(half * P // 2, (half + 1) * P // 2)
            nc.scalar.copy(
                out=grouped[:].rearrange("p (t m i) -> p m i t", t=PACK, i=PACK)[:, m],
                in_=raw[:].rearrange("p i (m t) -> p m i t", t=PACK)[:, m],
            )

        def round_weight(raw, tag):
            grouped = tenant(tag, "w_bf", [P, PACK * PASS], BF16)
            for half in range(2):
                round_half(grouped, raw, half)
            return grouped

        def quantise(codes, scales, grouped):
            nc.vector.quantize_mx(out=codes.bitcast(FP8X4), scales=scales, in_=grouped)

        tab_s = held("tab_s", T, U8)
        tab2_s = held("tab2_s", T, U8)
        tab3_s = tenant("K", "tab3_s", [P, T3], U8)
        w13_s_raw = tenant("M", "w13_s_raw", [P, 2 * H], U8)
        step_t = held("step_t", PACK, F32)
        for plane in (w13_s_raw, tab_s, tab3_s, tab2_s):
            nc.vector.memset(plane[:].bitcast(I32), 0)

        w1_raw = load_words("A", w1_words[0].bitcast(I32))
        w3_raw = load_words("B", words(w3_words[0]))
        nc.sync.dma_start(idx1[:], offs)
        tab_w = load_words("C", words(tab_words[0]))
        nc.sync.dma_start(idx3[:], offs3)
        tab3_w = load_words("D", tab3_words[0].bitcast(I32))
        nc.sync.dma_start(idx2[:], offs2)
        nc.sync.dma_start(out=step_t[:], in_=step.rearrange("(p t) -> p t", t=PACK))
        load_scale_rows(nc.sync, tab_s, tab_scales[0])
        load_scale_rows(nc.sync, tab3_s, tab3_scales[0])
        load_scale_rows(nc.gpsimd, w13_s_raw[:, 0:H], w1_scales[0])
        load_scale_rows(nc.gpsimd, w13_s_raw[:, H : 2 * H], w3_scales[0])
        for q in range(4):
            nc.gpsimd.dma_start(out=tab2_s[32 * q : 32 * q + 8, :].bitcast(I32), in_=tab2_scales[:, 4 * q : 4 * q + 4, :].bitcast(I32))

        w1_c = held("w1_c", 2 * H, U8)
        w3_c = held("w3_c", H, I32)
        v_w = held("v_w", S, U32)
        v2_w = [held("v2_w%d" % a, S, U32) for a in range(2)]
        v3_w = held("v3_w", S, U16)
        v_s = held("v_s", S, U8)
        v3_s = held("v3_s", S, U8)
        w2_c = {(b, a): held("w2_c%d%d" % (b, a), PASS, U32) for b in range(2) for a in range(2) if a + b > 0}
        w2_s = [[held("w2_s%d%d" % (b, a), PASS, U8) for a in range(2)] for b in range(2)]
        w4_s = [held("w4_s%d" % b, N, U8) for b in range(2)]
        w2_raw, tab2_w, w4_raw, meas_t = {}, {}, {}, {}

        nc.vector.tensor_copy(
            out=w1_c[:].bitcast(U16).rearrange("p (b t m) -> p b t m", b=2, t=PACK),
            in_=w1_raw[:].bitcast(U16).rearrange("p (b m t) -> p b t m", b=2, t=PACK),
        )
        w2_raw[0, 0] = load_weight("A", w2, 0, 0)
        nc.vector.tensor_copy(
            out=w3_c[:].rearrange("p (b t m i) -> p b m t i", b=2, t=PACK, i=LINE),
            in_=w3_raw[:].rearrange("p (b m i t) -> p b m t i", b=2, t=PACK, i=LINE),
        )
        tab2_w[0] = load_words("B", words(tab2_words[0]))
        gather(v_w[:], tab_w[:].bitcast(U32), idx1[:])
        w2_raw[0, 1] = load_weight("C", w2, 1, 0)
        gather(v3_w[:], tab3_w[:].bitcast(U16), idx3[:])
        tab2_w[1] = load_words("D", words(tab2_words[1]))
        gather(v_s[:], tab_s[:], idx1[:])
        w2_bf = round_weight(w2_raw[0, 0], "N")
        w2_raw[1, 0] = load_weight("A", w2, 0, 1)
        gather(v2_w[0][:], tab2_w[0][:].bitcast(U32), idx2[:])
        w2_raw[1, 1] = load_weight("B", w2, 1, 1)
        gather(v3_s[:], tab3_s[:], idx3[:])
        w13_s = tenant("K", "w13_s", [P, 2 * H], U8)
        nc.vector.tensor_copy(
            out=w13_s[:].rearrange("p (g t m) -> p g t m", g=2 * H // PASS, t=PACK),
            in_=w13_s_raw[:].rearrange("p (g m t) -> p g t m", g=2 * H // PASS, t=PACK),
        )
        w2_c[0, 0] = tenant("M", "w2_c", [P, PASS], U32)
        quantise(w2_c[0, 0][:], w2_s[0][0][:], w2_bf[:])
        w2_bf = round_weight(w2_raw[0, 1], "G")
        meas_t[0] = load_meas("C", 0)
        gather(v2_w[1][:], tab2_w[1][:].bitcast(U32), idx2[:])
        quantise(w2_c[0, 1][:], w2_s[0][1][:], w2_bf[:])
        w4_raw[0] = load_weight("G", w4, 0, 0)
        v2_s = tenant("N", "v2_s", [P, S], U8)
        for h in range(2):
            gather(v2_s[:, h * S // 2 : (h + 1) * S // 2], tab2_s[:], idx2[:, h * S // 32 : (h + 1) * S // 32])
        quantise(w2_c[1, 0][:], w2_s[1][0][:], round_weight(w2_raw[1, 0], step_tag(0))[:])
        meas_t[1] = load_meas("A", 1)
        quantise(w2_c[1, 1][:], w2_s[1][1][:], round_weight(w2_raw[1, 1], step_tag(1))[:])
        w4_raw[1] = load_weight("B", w4, 1, 0)

        z_s = [held("z_s%d" % c, 2 * CHUNK, U8) for c in range(CHUNKS)]
        y_s = held("y_s", S, U8)
        z_bf, z_c, y_bf, w4_bf, w4_c, y_tiles = {}, {}, {}, {}, {}, {}

        def woven(rows):
            return rows.rearrange("p t j -> p j t")

        def as_woven(flat):
            return flat.rearrange("p (j t) -> p j t", t=PACK)

        def paired(rows):
            return rows.rearrange("p (u e) j -> p u j e", e=2)

        def codes_tile(i, name, width):
            return tenant(step_tag(i), name, [P, width], U32)

        def products(i):
            c, b = divmod(i, 2)
            cols = slice(c * CHUNK, (c + 1) * CHUNK)
            seed = psum.tile([P, PACK, CHUNK], F32, name="seed", tag="seed", bufs=2)
            soil = psum.tile([P, PACK, CHUNK], F32, name="soil", tag="soil", bufs=2)
            rain = psum.tile([P, PACK, CHUNK], F32, name="rain", tag="rain", bufs=2)
            for t in range(PACK):
                r0 = b * PASS + t * P
                nc.tensor.matmul_mx(
                    out=seed[:, t, :], lhsT=w1_c[:, 2 * r0 : 2 * (r0 + P)].bitcast(FP4X4), lhsT_scale=w13_s[:, r0 : r0 + P],
                    rhs=v_w[:, cols].bitcast(FP8X4), rhs_scale=v_s[:, cols], start=True, stop=True,
                )
            for t in range(PACK):
                wc = slice(t * P, (t + 1) * P)
                for a in range(2):
                    nc.tensor.matmul_mx(
                        out=soil[:, t, :], lhsT=w2_c[b, a][:, wc].bitcast(FP8X4), lhsT_scale=w2_s[b][a][:, wc],
                        rhs=v2_w[a][:, cols].bitcast(FP8X4), rhs_scale=v2_s[4 * a : P, cols],
                        start=(a == 0), stop=(a == 1),
                    )
            for t in range(PACK):
                r0 = b * PASS + t * P
                nc.tensor.matmul_mx(
                    out=rain[:, t, :], lhsT=w3_c[:, r0 : r0 + P].bitcast(FP8X4), lhsT_scale=w13_s[:, H + r0 : H + r0 + P],
                    rhs=v3_w[:, cols].bitcast(FP4X4), rhs_scale=v3_s[:, cols], start=True, stop=True,
                )
            square = tenant(step_tag(i), "square", [P, PACK * CHUNK], F32)
            nc.scalar.activation(out=as_woven(square[:]), in_=woven(seed[:]), func=SQUARE)
            partial = shared.tile([P, PACK * CHUNK], F32, name="partial", tag="partial", bufs=2)
            nc.vector.tensor_tensor(out=as_woven(partial[:]), in0=woven(soil[:]), in1=as_woven(square[:]), op=MULT)
            minus = shared.tile([P, 2, CHUNK, 2], F32, name="minus", tag="minus", bufs=3)
            q, col = divmod(c * CHUNK, MEAS_COLS)
            nc.vector.tensor_tensor(out=minus[:], in0=paired(seed[:]), in1=paired(meas_t[q][:, b, :, col : col + CHUNK]), op=MULT)
            plus = shared.tile([P, PACK * CHUNK], F32, name="plus", tag="plus", bufs=3)
            nc.vector.tensor_tensor(out=as_woven(plus[:]), in0=woven(rain[:]), in1=as_woven(partial[:]), op=MULT)
            if b == 0:
                z_bf[c] = shared.tile([P, 2 * PASS], BF16, name="z_bf", tag="z_bf", bufs=3, align_bytes=64)
            return lambda engine: engine.tensor_tensor(
                out=z_bf[c][:, b * PASS : (b + 1) * PASS].rearrange("p (j u e) -> p j u e", u=2, e=2),
                in0=plus[:].rearrange("p (j u e) -> p j u e", u=2, e=2),
                in1=minus[:].rearrange("p u j e -> p j u e"), op=SUB,
            )

        store_of = {}
        for n, width in enumerate(Y_STORES):
            first = sum(Y_STORES[:n])
            for j in range(first, first + width, CHUNK):
                store_of[j] = (first, width)

        def quantise_z(i, c):
            z_c[c] = codes_tile(i, "z_c", 2 * CHUNK)
            quantise(z_c[c][:], z_s[c][:], z_bf[c][:])

        def make_y(c):
            j = c * CHUNK
            first, width = store_of[j]
            if j == first:
                y_tiles[first] = shared.tile([P, PACK, width], F32, name="y", tag="y", bufs=2)
            y = y_tiles[first][:, :, j - first : j - first + CHUNK]
            bank = psum.tile([P, PACK, CHUNK], F32, name="y_bank", tag="y_bank", bufs=2)
            for t in range(PACK):
                wc = slice(t * P, (t + 1) * P)
                for b in range(2):
                    zc = slice(b * CHUNK, (b + 1) * CHUNK)
                    nc.tensor.matmul_mx(
                        out=bank[:, t, :], lhsT=w4_c[b][:, wc].bitcast(FP8X4), lhsT_scale=w4_s[b][:, wc],
                        rhs=z_c[c][:, zc].bitcast(FP8X4), rhs_scale=z_s[c][:, zc],
                        start=(b == 0), stop=(b == 1),
                    )
            y_bf[c] = shared.tile([P, PACK * CHUNK], BF16, name="y_bf", tag="y_bf", bufs=3, align_bytes=64)
            if c == CHUNKS - 1:
                nc.vector.tensor_tensor(out=y, in0=bank[:], in1=step_t[:].unsqueeze(2).to_broadcast([P, PACK, CHUNK]), op=MULT)
            else:
                for t in range(PACK):
                    nc.scalar.activation(out=y[:, t, :], in_=bank[:, t, :], func=COPY, scale=step_t[:, t : t + 1])
            if j + CHUNK == first + width:
                nc.sync.dma_start(out=out_0[:, first : first + width].rearrange("(p t) j -> p t j", t=PACK), in_=y_tiles[first][:])
            return y

        def round_y(c, y):
            dst = y_bf[c][:].rearrange("p (g i t) -> p g t i", i=LINE, t=PACK)
            src = y.rearrange("p t (g i) -> p g t i", i=LINE)
            if c == CHUNKS - 1:
                nc.vector.tensor_copy(out=dst, in_=src)
            else:
                nc.scalar.copy(out=dst, in_=src)

        def quantise_y(i, c):
            cols = slice(c * CHUNK, (c + 1) * CHUNK)
            y_c = codes_tile(i, "y_c", CHUNK)
            quantise(y_c[:], y_s[:, cols], y_bf[c][:])
            nc.sync.dma_start(out=words(out_1[0])[:, cols], in_=y_c[:].bitcast(I32))

        for i in range(STEPS):
            c, b = divmod(i, 2)
            subtract = products(i)
            if i < STEPS - 1:
                subtract(nc.gpsimd)
            if c < 2:
                if b == 0:
                    w4_bf[c] = tenant(step_tag(c), "w_bf", [P, PACK * PASS], BF16)
                round_half(w4_bf[c], w4_raw[c], b)
                if b == 1:
                    meas_t[2 + c] = load_meas("GB"[c], 2 + c)
            if b == 0 and c - 1 in w4_bf:
                w4_c[c - 1] = codes_tile(i, "w4_c", N)
                quantise(w4_c[c - 1][:], w4_s[c - 1][:], w4_bf[c - 1][:])
            if b == 1 and c >= 1:
                quantise_z(i, c - 1)
            if (c, b) == (2, 0):
                round_y(0, make_y(0))
            if b == 1 and c >= 2:
                round_y(c - 1, make_y(c - 1))
            if b == 0 and c >= 3:
                quantise_y(i, c - 3)

        subtract(nc.vector)
        quantise_y(STEPS, CHUNKS - 3)
        quantise_z(STEPS + 1, CHUNKS - 1)
        y_last = make_y(CHUNKS - 1)
        quantise_y(STEPS + 2, CHUNKS - 2)
        round_y(CHUNKS - 1, y_last)
        quantise_y(STEPS + 3, CHUNKS - 1)
        for q in range(4):
            queue = nc.scalar if q % 2 else nc.sync
            queue.dma_start(out=out_2[0, 4 * q : 4 * q + 4, :].bitcast(I32), in_=y_s[32 * q : 32 * q + 4, :].bitcast(I32))
